import numpy as np, ml_dtypes
CORES = [0,11,22,25,36,47,50,61,64,75,86,89]
N = 12
G1 = [0,1,2,3,4,5,6,7,8,9,10,11]
G2 = [0,2,4,6,8,10]
G3 = [1,3,5,7,9,11]
def setup_inputs(rng):
    return {"x1": rng.standard_normal((N, 128, 4), dtype=np.float32), "x2": rng.standard_normal((N, 128, 32), dtype=np.float32), "x3": rng.standard_normal((N, 128, 1024), dtype=np.float32).astype(ml_dtypes.bfloat16)}
def reference(x1, x2, x3):
    out = {}
    y = np.full((N, 128, 4), np.nan, x1.dtype)
    s = x1[G1].sum(axis=0, dtype=np.float64).astype(x1.dtype)
    for r in G1:
        y[r] = s
    out["y1"] = y
    y = np.full((N, 128, 192), np.nan, x2.dtype)
    s = np.concatenate([x2[r] for r in G2], axis=1)
    for r in G2:
        y[r] = s
    out["y2"] = y
    y = np.full((N, 128, 1024), np.nan, x3.dtype)
    for i, r in enumerate(G3):
        y[G3[(i + 1) % 6]] = x3[r]
    out["y3"] = y
    return out

@@ -1,0 +1,172 @@
+from concourse.bass import DstId, RemoteDMATransfer
+
+NSIM = 96
+N = 12
+N2 = 6
+K3 = 2
+W2 = 32
+R3 = 128 // K3
+
+SCRATCH = {
+    "s1": ("dram", [128, 4], "float32"),
+    "in1": ("dram", [N + 1, 128, 4], "float32"),
+    "r1": ("dram", [128, 4], "float32"),
+    "s2": ("dram", [128, W2], "float32"),
+    "l2": ("dram", [N2, 128, W2], "float32"),
+    "s3": ("dram", [K3, 128, 1024 // K3], "bfloat16"),
+    "l3": ("dram", [K3, 128, 1024 // K3], "bfloat16"),
+}
+SEMAPHORES = (["ld1", "ld2", "a1", "b1", "c1", "snt", "st_sync", "st_scalar"]
+              + ["a2_%d" % j for j in range(N2)]
+              + ["ld3_%d" % k for k in range(K3)] + ["a3_%d" % k for k in range(K3)])
+
+
+def _bits(m):
+    return bin(m).count("1")
+
+
+def _plan(T, topo):
+    cores = list(T.cores)
+    g1 = [cores[r] for r in T.tables["G1"]]
+    g2 = [cores[r] for r in T.tables["G2"]]
+    g3 = [cores[r] for r in T.tables["G3"]]
+    planes = []
+    for c in g1:
+        for pl in planes:
+            a, b = topo.chip(pl[0]), topo.chip(c)
+            if a == b or topo.same_plane(a, b):
+                pl.append(c)
+                break
+        else:
+            planes.append([c])
+    load = {}
+
+    def bulk(src, dst, nbytes):
+        if topo.chip(src) != topo.chip(dst):
+            for key in (("out", topo.chip(src), topo.die(src)), ("in", topo.chip(dst), topo.die(src))):
+                load[key] = load.get(key, 0) + nbytes
+
+    for i, c in enumerate(g3):
+        bulk(c, g3[(i + 1) % len(g3)], 128 * 1024 * 2)
+    for c in g2:
+        for d in g2:
+            if d != c:
+                bulk(c, d, 128 * W2 * 4)
+
+    def cands(x):
+        pl, other = planes[x], planes[1 - x]
+        out = []
+        for c in range(NSIM):
+            a = topo.chip(c)
+            if c in cores or not topo.may_write(c, other[0]):
+                continue
+            if not (a == topo.chip(pl[0]) or topo.same_plane(a, topo.chip(pl[0]))):
+                continue
+            cost = load.get(("out", a, topo.die(c)), 0)
+            cost += sum(load.get(("in", topo.chip(m), topo.die(c)), 0) for m in pl if topo.chip(m) != a)
+            out.append((cost, c))
+        return out
+
+    best = None
+    for ca, a in cands(0):
+        for cb, b in cands(1):
+            if topo.mates(topo.chip(a), topo.chip(b)) and (best is None or (ca + cb, a, b) < best):
+                best = (ca + cb, a, b)
+    return planes, [best[1], best[2]], g2, g3
+
+
+def rank_program(g, core, T, topo):
+    planes, roots, g2, g3 = _plan(T, topo)
+    sem = T.sem
+
+    def dst(c):
+        rid, pid, _ = topo.addr(c)
+        return DstId(rid=rid, pnc=pid)
+
+    def fan_mask(src, dsts):
+        m = topo.mask(src, dsts[0])
+        for d in dsts[1:]:
+            m &= topo.mask(src, d)
+        return m
+
+    if core in roots:
+        x = roots.index(core)
+        pl, other = planes[x], roots[1 - x]
+        n = len(pl)
+        g.wait_ge(sem.a1, sum(_bits(topo.mask(m, core)) for m in pl))
+        m1 = topo.mask(core, other)
+        g.remote_dma_fused([RemoteDMATransfer(
+            dst_ids=[dst(other)], dma_engine_mask=m1, remote_sem=sem.b1,
+            srcs=[T.in1[j] for j in range(n)], dsts=[T.in1[len(planes[1 - x])]], alu_op=1)], local_sem=sem.snt)
+        g.wait_ge(sem.b1, _bits(topo.mask(other, core)))
+        m2 = fan_mask(core, pl)
+        g.remote_dma_fused([RemoteDMATransfer(
+            dst_ids=[dst(m) for m in pl], dma_engine_mask=m2, remote_sem=sem.c1,
+            srcs=[T.in1[j] for j in range(n + 1)], dsts=[T.r1[:] for m in pl], alu_op=1)], local_sem=sem.snt)
+        g.wait_ge(sem.snt, _bits(m1) + _bits(m2))
+        return
+
+    if T.rank_of(core) is None:
+        return
+
+    sent = 0
+    done = {"sync": 0, "scalar": 0}
+    queue = {"sync": g.sync, "scalar": g.scalar}
+
+    def store(q, out, in_):
+        queue[q].dma_start(out, in_).then_inc(sem["st_" + q], 16)
+        done[q] += 16
+
+    x = 0 if core in planes[0] else 1
+    root = roots[x]
+
+    g.sync.dma_start(T.s1[:], T.x1[:]).then_inc(sem.ld1, 16)
+    if core in g2:
+        i2 = g2.index(core)
+        g.scalar.dma_start(T.s2[:], T.x2[:]).then_inc(sem.ld2, 16)
+        store("scalar", T.y2[:, W2 * i2:W2 * (i2 + 1)], T.x2[:])
+    if core in g3:
+        for k in range(K3):
+            q = g.scalar if k % 2 == 0 else g.sync
+            q.dma_start(T.s3[k], T.x3[R3 * k:R3 * (k + 1), :]).then_inc(sem["ld3_%d" % k], 16)
+
+    rid, pid, _ = topo.addr(root)
+    m = topo.mask(core, root)
+    g.wait_ge(sem.ld1, 16)
+    g.remote_dma(T.in1[planes[x].index(core)], T.s1[:], sem.a1, sem.snt, pid, rid, m)
+    sent += _bits(m)
+    if core in g2:
+        others = [g2[(i2 + k) % len(g2)] for k in range(1, len(g2))]
+        m = fan_mask(core, others)
+        g.wait_ge(sem.ld2, 16)
+        g.remote_dma_fused([RemoteDMATransfer(
+            dst_ids=[dst(d) for d in others], dma_engine_mask=m, remote_sem=sem["a2_%d" % i2],
+            src=T.s2[:], dsts=[T.l2[i2] for d in others], alu_op=0)], local_sem=sem.snt)
+        sent += _bits(m)
+    if core in g3:
+        i3 = g3.index(core)
+        nxt, prv = g3[(i3 + 1) % len(g3)], g3[(i3 - 1) % len(g3)]
+        rid, pid, _ = topo.addr(nxt)
+        m = topo.mask(core, nxt)
+        for k in range(K3):
+            g.wait_ge(sem["ld3_%d" % k], 16)
+            g.remote_dma(T.l3[k], T.s3[k], sem["a3_%d" % k], sem.snt, pid, rid, m)
+            sent += _bits(m)
+
+    if core in g2:
+        for k in range(1, len(g2)):
+            j = (i2 - k) % len(g2)
+            q = "scalar" if k % 2 == 1 else "sync"
+            queue[q].wait_ge(sem["a2_%d" % j], _bits(fan_mask(g2[j], [d for d in g2 if d != g2[j]])))
+            store(q, T.y2[:, W2 * j:W2 * (j + 1)], T.l2[j])
+    if core in g3:
+        for k in range(K3):
+            g.scalar.wait_ge(sem["a3_%d" % k], _bits(topo.mask(prv, core)))
+            store("scalar", T.y3[R3 * k:R3 * (k + 1), :], T.l3[k])
+    g.sync.wait_ge(sem.c1, _bits(fan_mask(root, planes[x])))
+    store("sync", T.y1[:], T.r1[:])
+
+    g.wait_ge(sem.snt, sent)
+    for q in ("sync", "scalar"):
+        if done[q]:
+            queue[q].wait_ge(sem["st_" + q], done[q])

@@ -9,7 +9,8 @@ R3 = 128 // K3
 
 SCRATCH = {
     "s1": ("dram", [128, 4], "float32"),
-    "in1": ("dram", [N + 1, 128, 4], "float32"),
+    "in1": ("dram", [N, 128, 4], "float32"),
+    "p1": ("dram", [2, 128, 4], "float32"),
     "r1": ("dram", [128, 4], "float32"),
     "s2": ("dram", [128, W2], "float32"),
     "l2": ("dram", [N2, 128, W2], "float32"),
@@ -23,6 +24,12 @@ SEMAPHORES = (["ld1", "ld2", "a1", "b1", "c1", "snt", "st_sync", "st_scalar"]
 
 def _bits(m):
     return bin(m).count("1")
+
+
+def _halves(m):
+    eng = [1 << b for b in range(m.bit_length()) if (m >> b) & 1]
+    h = len(eng) // 2
+    return [sum(eng[:h]), sum(eng[h:])]
 
 
 def _plan(T, topo):
@@ -54,13 +61,11 @@ def _plan(T, topo):
                 bulk(c, d, 128 * W2 * 4)
 
     def cands(x):
-        pl, other = planes[x], planes[1 - x]
+        pl = planes[x]
         out = []
         for c in range(NSIM):
             a = topo.chip(c)
-            if c in cores or not topo.may_write(c, other[0]):
-                continue
-            if not (a == topo.chip(pl[0]) or topo.same_plane(a, topo.chip(pl[0]))):
+            if c in cores or not (a == topo.chip(pl[0]) or topo.same_plane(a, topo.chip(pl[0]))):
                 continue
             cost = load.get(("out", a, topo.die(c)), 0)
             cost += sum(load.get(("in", topo.chip(m), topo.die(c)), 0) for m in pl if topo.chip(m) != a)
@@ -72,11 +77,16 @@ def _plan(T, topo):
         for cb, b in cands(1):
             if topo.mates(topo.chip(a), topo.chip(b)) and (best is None or (ca + cb, a, b) < best):
                 best = (ca + cb, a, b)
-    return planes, [best[1], best[2]], g2, g3
+    fins = [best[1], best[2]]
+    roots = []
+    for x in (0, 1):
+        roots.append([c for c in range(NSIM) if topo.chip(c) == topo.chip(fins[x]) and c not in cores
+                      and c != fins[x] and topo.may_write(c, fins[1 - x])][0])
+    return planes, roots, fins, g2, g3
 
 
 def rank_program(g, core, T, topo):
-    planes, roots, g2, g3 = _plan(T, topo)
+    planes, roots, fins, g2, g3 = _plan(T, topo)
     sem = T.sem
 
     def dst(c):
@@ -91,19 +101,25 @@ def rank_program(g, core, T, topo):
 
     if core in roots:
         x = roots.index(core)
-        pl, other = planes[x], roots[1 - x]
-        n = len(pl)
+        pl = planes[x]
         g.wait_ge(sem.a1, sum(_bits(topo.mask(m, core)) for m in pl))
-        m1 = topo.mask(core, other)
+        m1 = fan_mask(core, fins)
         g.remote_dma_fused([RemoteDMATransfer(
-            dst_ids=[dst(other)], dma_engine_mask=m1, remote_sem=sem.b1,
-            srcs=[T.in1[j] for j in range(n)], dsts=[T.in1[len(planes[1 - x])]], alu_op=1)], local_sem=sem.snt)
-        g.wait_ge(sem.b1, _bits(topo.mask(other, core)))
-        m2 = fan_mask(core, pl)
+            dst_ids=[dst(f) for f in fins], dma_engine_mask=m1, remote_sem=sem.b1,
+            srcs=[T.in1[j] for j in range(len(pl))], dsts=[T.p1[x] for f in fins], alu_op=1)], local_sem=sem.snt)
+        g.wait_ge(sem.snt, _bits(m1))
+        return
+    if core in fins:
+        x = fins.index(core)
+        pl = planes[x]
+        g.wait_ge(sem.b1, sum(_bits(fan_mask(r, fins)) for r in roots))
+        hm = _halves(fan_mask(core, pl))
+        h = len(pl) // 2
         g.remote_dma_fused([RemoteDMATransfer(
-            dst_ids=[dst(m) for m in pl], dma_engine_mask=m2, remote_sem=sem.c1,
-            srcs=[T.in1[j] for j in range(n + 1)], dsts=[T.r1[:] for m in pl], alu_op=1)], local_sem=sem.snt)
-        g.wait_ge(sem.snt, _bits(m1) + _bits(m2))
+            dst_ids=[dst(m) for m in part], dma_engine_mask=mk, remote_sem=sem.c1,
+            srcs=[T.p1[0], T.p1[1]], dsts=[T.r1[:] for m in part], alu_op=1)
+            for part, mk in ((pl[:h], hm[0]), (pl[h:], hm[1]))], local_sem=sem.snt)
+        g.wait_ge(sem.snt, _bits(hm[0]) + _bits(hm[1]))
         return
 
     if T.rank_of(core) is None:
@@ -163,7 +179,7 @@ def rank_program(g, core, T, topo):
         for k in range(K3):
             g.scalar.wait_ge(sem["a3_%d" % k], _bits(topo.mask(prv, core)))
             store("scalar", T.y3[R3 * k:R3 * (k + 1), :], T.l3[k])
-    g.sync.wait_ge(sem.c1, _bits(fan_mask(root, planes[x])))
+    g.sync.wait_ge(sem.c1, _bits(_halves(fan_mask(fins[x], planes[x]))[0]))
     store("sync", T.y1[:], T.r1[:])
 
     g.wait_ge(sem.snt, sent)

@@ -3,9 +3,10 @@ from concourse.bass import DstId, RemoteDMATransfer
 NSIM = 96
 N = 12
 N2 = 6
-K3 = 2
 W2 = 32
-R3 = 128 // K3
+ROWS3 = [32, 64, 32]
+K3 = 3
+OFF3 = [0, 32, 96, 128]
 
 SCRATCH = {
     "s1": ("dram", [128, 4], "float32"),
@@ -14,8 +15,9 @@ SCRATCH = {
     "r1": ("dram", [128, 4], "float32"),
     "s2": ("dram", [128, W2], "float32"),
     "l2": ("dram", [N2, 128, W2], "float32"),
-    "s3": ("dram", [K3, 128, 1024 // K3], "bfloat16"),
-    "l3": ("dram", [K3, 128, 1024 // K3], "bfloat16"),
+    "s3_0": ("dram", [128, 8 * ROWS3[0]], "bfloat16"), "l3_0": ("dram", [128, 8 * ROWS3[0]], "bfloat16"),
+    "s3_1": ("dram", [128, 8 * ROWS3[1]], "bfloat16"), "l3_1": ("dram", [128, 8 * ROWS3[1]], "bfloat16"),
+    "s3_2": ("dram", [128, 8 * ROWS3[2]], "bfloat16"), "l3_2": ("dram", [128, 8 * ROWS3[2]], "bfloat16"),
 }
 SEMAPHORES = (["ld1", "ld2", "a1", "b1", "c1", "snt", "st_sync", "st_scalar"]
               + ["a2_%d" % j for j in range(N2)]
@@ -144,7 +146,7 @@ def rank_program(g, core, T, topo):
     if core in g3:
         for k in range(K3):
             q = g.scalar if k % 2 == 0 else g.sync
-            q.dma_start(T.s3[k], T.x3[R3 * k:R3 * (k + 1), :]).then_inc(sem["ld3_%d" % k], 16)
+            q.dma_start(T["s3_%d" % k][:], T.x3[OFF3[k]:OFF3[k + 1], :]).then_inc(sem["ld3_%d" % k], 16)
 
     rid, pid, _ = topo.addr(root)
     m = topo.mask(core, root)
@@ -166,7 +168,7 @@ def rank_program(g, core, T, topo):
         m = topo.mask(core, nxt)
         for k in range(K3):
             g.wait_ge(sem["ld3_%d" % k], 16)
-            g.remote_dma(T.l3[k], T.s3[k], sem["a3_%d" % k], sem.snt, pid, rid, m)
+            g.remote_dma(T["l3_%d" % k][:], T["s3_%d" % k][:], sem["a3_%d" % k], sem.snt, pid, rid, m)
             sent += _bits(m)
 
     if core in g2:
@@ -178,7 +180,7 @@ def rank_program(g, core, T, topo):
     if core in g3:
         for k in range(K3):
             g.scalar.wait_ge(sem["a3_%d" % k], _bits(topo.mask(prv, core)))
-            store("scalar", T.y3[R3 * k:R3 * (k + 1), :], T.l3[k])
+            store("scalar", T.y3[OFF3[k]:OFF3[k + 1], :], T["l3_%d" % k][:])
     g.sync.wait_ge(sem.c1, _bits(_halves(fan_mask(fins[x], planes[x]))[0]))
     store("sync", T.y1[:], T.r1[:])
 

from concourse.bass import DstId, RemoteDMATransfer

NSIM = 96
N = 12
N2 = 6
W2 = 32
ROWS3 = [32, 64, 32]
K3 = 3
OFF3 = [0, 32, 96, 128]

SCRATCH = {
    "s1": ("dram", [128, 4], "float32"),
    "in1": ("dram", [N, 128, 4], "float32"),
    "p1": ("dram", [2, 128, 4], "float32"),
    "r1": ("dram", [128, 4], "float32"),
    "s2": ("dram", [128, W2], "float32"),
    "l2": ("dram", [N2, 128, W2], "float32"),
    "s3_0": ("dram", [128, 8 * ROWS3[0]], "bfloat16"), "l3_0": ("dram", [128, 8 * ROWS3[0]], "bfloat16"),
    "s3_1": ("dram", [128, 8 * ROWS3[1]], "bfloat16"), "l3_1": ("dram", [128, 8 * ROWS3[1]], "bfloat16"),
    "s3_2": ("dram", [128, 8 * ROWS3[2]], "bfloat16"), "l3_2": ("dram", [128, 8 * ROWS3[2]], "bfloat16"),
}
SEMAPHORES = (["ld1", "ld2", "a1", "b1", "c1", "snt", "st_sync", "st_scalar"]
              + ["a2_%d" % j for j in range(N2)]
              + ["ld3_%d" % k for k in range(K3)] + ["a3_%d" % k for k in range(K3)])


def _bits(m):
    return bin(m).count("1")


def _halves(m):
    eng = [1 << b for b in range(m.bit_length()) if (m >> b) & 1]
    h = len(eng) // 2
    return [sum(eng[:h]), sum(eng[h:])]


def _plan(T, topo):
    cores = list(T.cores)
    g1 = [cores[r] for r in T.tables["G1"]]
    g2 = [cores[r] for r in T.tables["G2"]]
    g3 = [cores[r] for r in T.tables["G3"]]
    planes = []
    for c in g1:
        for pl in planes:
            a, b = topo.chip(pl[0]), topo.chip(c)
            if a == b or topo.same_plane(a, b):
                pl.append(c)
                break
        else:
            planes.append([c])
    load = {}

    def bulk(src, dst, nbytes):
        if topo.chip(src) != topo.chip(dst):
            for key in (("out", topo.chip(src), topo.die(src)), ("in", topo.chip(dst), topo.die(src))):
                load[key] = load.get(key, 0) + nbytes

    for i, c in enumerate(g3):
        bulk(c, g3[(i + 1) % len(g3)], 128 * 1024 * 2)
    for c in g2:
        for d in g2:
            if d != c:
                bulk(c, d, 128 * W2 * 4)

    def cands(x):
        pl = planes[x]
        out = []
        for c in range(NSIM):
            a = topo.chip(c)
            if c in cores or not (a == topo.chip(pl[0]) or topo.same_plane(a, topo.chip(pl[0]))):
                continue
            cost = load.get(("out", a, topo.die(c)), 0)
            cost += sum(load.get(("in", topo.chip(m), topo.die(c)), 0) for m in pl if topo.chip(m) != a)
            out.append((cost, c))
        return out

    best = None
    for ca, a in cands(0):
        for cb, b in cands(1):
            if topo.mates(topo.chip(a), topo.chip(b)) and (best is None or (ca + cb, a, b) < best):
                best = (ca + cb, a, b)
    fins = [best[1], best[2]]
    roots = []
    for x in (0, 1):
        roots.append([c for c in range(NSIM) if topo.chip(c) == topo.chip(fins[x]) and c not in cores
                      and c != fins[x] and topo.may_write(c, fins[1 - x])][0])
    return planes, roots, fins, g2, g3


def rank_program(g, core, T, topo):
    planes, roots, fins, g2, g3 = _plan(T, topo)
    sem = T.sem

    def dst(c):
        rid, pid, _ = topo.addr(c)
        return DstId(rid=rid, pnc=pid)

    def fan_mask(src, dsts):
        m = topo.mask(src, dsts[0])
        for d in dsts[1:]:
            m &= topo.mask(src, d)
        return m

    if core in roots:
        x = roots.index(core)
        pl = planes[x]
        g.wait_ge(sem.a1, sum(_bits(topo.mask(m, core)) for m in pl))
        m1 = fan_mask(core, fins)
        g.remote_dma_fused([RemoteDMATransfer(
            dst_ids=[dst(f) for f in fins], dma_engine_mask=m1, remote_sem=sem.b1,
            srcs=[T.in1[j] for j in range(len(pl))], dsts=[T.p1[x] for f in fins], alu_op=1)], local_sem=sem.snt)
        g.wait_ge(sem.snt, _bits(m1))
        return
    if core in fins:
        x = fins.index(core)
        pl = planes[x]
        g.wait_ge(sem.b1, sum(_bits(fan_mask(r, fins)) for r in roots))
        hm = _halves(fan_mask(core, pl))
        h = len(pl) // 2
        g.remote_dma_fused([RemoteDMATransfer(
            dst_ids=[dst(m) for m in part], dma_engine_mask=mk, remote_sem=sem.c1,
            srcs=[T.p1[0], T.p1[1]], dsts=[T.r1[:] for m in part], alu_op=1)
            for part, mk in ((pl[:h], hm[0]), (pl[h:], hm[1]))], local_sem=sem.snt)
        g.wait_ge(sem.snt, _bits(hm[0]) + _bits(hm[1]))
        return

    if T.rank_of(core) is None:
        return

    sent = 0
    done = {"sync": 0, "scalar": 0}
    queue = {"sync": g.sync, "scalar": g.scalar}

    def store(q, out, in_):
        queue[q].dma_start(out, in_).then_inc(sem["st_" + q], 16)
        done[q] += 16

    x = 0 if core in planes[0] else 1
    root = roots[x]

    g.sync.dma_start(T.s1[:], T.x1[:]).then_inc(sem.ld1, 16)
    if core in g2:
        i2 = g2.index(core)
        g.scalar.dma_start(T.s2[:], T.x2[:]).then_inc(sem.ld2, 16)
        store("scalar", T.y2[:, W2 * i2:W2 * (i2 + 1)], T.x2[:])
    if core in g3:
        for k in range(K3):
            q = g.scalar if k % 2 == 0 else g.sync
            q.dma_start(T["s3_%d" % k][:], T.x3[OFF3[k]:OFF3[k + 1], :]).then_inc(sem["ld3_%d" % k], 16)

    rid, pid, _ = topo.addr(root)
    m = topo.mask(core, root)
    g.wait_ge(sem.ld1, 16)
    g.remote_dma(T.in1[planes[x].index(core)], T.s1[:], sem.a1, sem.snt, pid, rid, m)
    sent += _bits(m)
    if core in g2:
        others = [g2[(i2 + k) % len(g2)] for k in range(1, len(g2))]
        m = fan_mask(core, others)
        g.wait_ge(sem.ld2, 16)
        g.remote_dma_fused([RemoteDMATransfer(
            dst_ids=[dst(d) for d in others], dma_engine_mask=m, remote_sem=sem["a2_%d" % i2],
            src=T.s2[:], dsts=[T.l2[i2] for d in others], alu_op=0)], local_sem=sem.snt)
        sent += _bits(m)
    if core in g3:
        i3 = g3.index(core)
        nxt, prv = g3[(i3 + 1) % len(g3)], g3[(i3 - 1) % len(g3)]
        rid, pid, _ = topo.addr(nxt)
        m = topo.mask(core, nxt)
        for k in range(K3):
            g.wait_ge(sem["ld3_%d" % k], 16)
            g.remote_dma(T["l3_%d" % k][:], T["s3_%d" % k][:], sem["a3_%d" % k], sem.snt, pid, rid, m)
            sent += _bits(m)

    if core in g2:
        for k in range(1, len(g2)):
            j = (i2 - k) % len(g2)
            q = "scalar" if k % 2 == 1 else "sync"
            queue[q].wait_ge(sem["a2_%d" % j], _bits(fan_mask(g2[j], [d for d in g2 if d != g2[j]])))
            store(q, T.y2[:, W2 * j:W2 * (j + 1)], T.l2[j])
    if core in g3:
        for k in range(K3):
            g.scalar.wait_ge(sem["a3_%d" % k], _bits(topo.mask(prv, core)))
            store("scalar", T.y3[OFF3[k]:OFF3[k + 1], :], T["l3_%d" % k][:])
    g.sync.wait_ge(sem.c1, _bits(_halves(fan_mask(fins[x], planes[x]))[0]))
    store("sync", T.y1[:], T.r1[:])

    g.wait_ge(sem.snt, sent)
    for q in ("sync", "scalar"):
        if done[q]:
            queue[q].wait_ge(sem["st_" + q], done[q])
